import numpy as np
import ml_dtypes


def mxq(x, axis, fmt="e4m3"):
    dtype, down = {"e4m3": (ml_dtypes.float8_e4m3fn, 7), "e5m2": (ml_dtypes.float8_e5m2, 14)}[fmt]
    v = np.moveaxis(np.asarray(x, np.float32).astype(ml_dtypes.bfloat16).astype(np.float64), axis, -1)
    blocks = v.reshape(v.shape[:-1] + (-1, 32))
    amax = np.abs(blocks).max(-1, keepdims=True)
    byte = np.maximum(np.where(amax > 0, np.frexp(amax)[1] - 1 + 127, 0) - down, 1)
    scale = np.exp2(byte - 127.0)
    codes = (blocks / scale).astype(np.float32).astype(dtype).astype(np.float64)
    return np.moveaxis((codes * scale).reshape(v.shape), -1, axis)


WIDE = False


def mx_kscale(k):
    if not WIDE:
        return np.ones(k)
    levels = np.array([10, -10, 5, -5, 0])
    if k % 512:
        return np.exp2(np.random.permutation(np.resize(levels, k // 32))).repeat(32)
    a = np.empty((k // 512, 16))
    for p in range(k // 512):
        a[p, :8] = np.random.permutation(np.resize(levels, 8))
        for g in range(8):
            far = levels[np.abs(levels - a[p, g]) >= 10]
            a[p, g + 8] = far[np.random.randint(len(far))]
    return np.exp2(a.ravel()).repeat(32)


def f64(x):
    return np.asarray(x).astype(np.float64)


def striped(idx):
    return np.tile(np.asarray(idx).reshape(-1, 16).T, (8, 1)).astype(np.uint16)


def unstriped(offs):
    return offs[:16].T.reshape(-1).astype(np.int64)


def striped8(idx):
    return np.asarray(idx).reshape(8, -1, 16).transpose(0, 2, 1).reshape(128, -1).astype(np.uint16)


def unstriped8(offs):
    return offs.reshape(8, 16, -1).transpose(0, 2, 1).reshape(8, -1).astype(np.int64)


def pick8(x, idx, run):
    r = np.arange(len(x))
    return x[r[:, None], idx[r % (8 * run) // run]]


E2M1 = np.array([0.0, 0.5, 1.0, 1.5, 2.0, 3.0, 4.0, 6.0, -0.0, -0.5, -1.0, -1.5, -2.0, -3.0, -4.0, -6.0])


def pack_weight(w, fmt):
    k, n = w.shape
    w = f64(np.asarray(w, np.float32).astype(ml_dtypes.bfloat16)).reshape(k // 32, 32, n)
    amax = np.abs(w).max(1)
    if fmt == "e4m3":
        byte = np.frexp(amax)[1] - 1 + 127 - 7
    else:
        mant, ex = np.frexp(amax / 6.0)
        byte = np.where(mant > 0.5, ex, ex - 1) + 127
    byte = np.clip(np.where(amax > 0, byte, 1), 1, 254)
    scaled = (w * np.exp2(127.0 - byte)[:, None, :]).reshape(k, n).astype(np.float32)
    by_word = np.ascontiguousarray(scaled.reshape(k // 512, 128, 4, n).transpose(0, 1, 3, 2))
    if fmt == "e4m3":
        words = by_word.astype(ml_dtypes.float8_e4m3fn).view(np.uint8)
    else:
        c = by_word.astype(ml_dtypes.float4_e2m1fn).view(np.uint8) & 0xF
        words = (c[..., 0::2] | (c[..., 1::2] << 4)).reshape(k // 512, 128, 2 * n)
    return np.ascontiguousarray(words), np.ascontiguousarray(byte.astype(np.uint8).reshape(k // 512, 16, n))


def unpack_weight(words, scales, fmt):
    g, _, n = scales.shape
    words = np.ascontiguousarray(words).reshape(g, 128, n, -1)
    if fmt == "e4m3":
        vals = words.view(ml_dtypes.float8_e4m3fn).astype(np.float64)
    else:
        nib = np.empty((g, 128, n, 4), np.uint8)
        nib[..., 0::2] = words & 0xF
        nib[..., 1::2] = words >> 4
        vals = E2M1[nib]
    vals = vals * np.repeat(np.exp2(scales.astype(np.float64) - 127.0), 8, axis=1)[..., None]
    return vals.transpose(0, 1, 3, 2).reshape(g * 512, n)


K, J, R, T, O, N, E, U = 512, 512, 512, 1024, 256, 256, 128, 256


def setup_inputs():
    n = np.random.standard_normal
    idx = np.random.permutation(T)[:J]
    idx2 = np.stack([np.random.permutation(J)[:O] for _ in range(8)])
    idx3 = np.stack([np.random.permutation(J)[:O] for _ in range(8)])
    idx4 = np.stack([np.random.permutation(O)[:E] for _ in range(8)])
    idx5 = np.stack([np.random.permutation(O)[:E] for _ in range(8)])
    idx6 = np.stack([np.random.permutation(U)[:E] for _ in range(8)])
    idx7 = np.stack([np.random.permutation(U)[:E] for _ in range(8)])
    fk = mx_kscale(K)
    fr = mx_kscale(R)
    xtp = pack_weight(n((K, T)) * fk[:, None], "e4m3")
    wp = pack_weight(n((K, R)) * 1 / np.sqrt(K) / fk[:, None] * fr, "e2m1")
    w2p = pack_weight(n((K, R)) * 1 / np.sqrt(K) / fk[:, None] * fr, "e4m3")
    wbp = pack_weight(n((R, N)) * 1 / np.sqrt(R) / fr[:, None], "e4m3")
    return {
        "xt_words": xtp[0],
        "xt_scales": xtp[1],
        "w_words": wp[0],
        "w_scales": wp[1],
        "w2_words": w2p[0],
        "w2_scales": w2p[1],
        "sa": (np.random.uniform(0.5, 1.6, (R, 1))).astype(np.float32),
        "sb": (np.random.uniform(0.5, 1.6, (R, 1))).astype(np.float32),
        "wb_words": wbp[0],
        "wb_scales": wbp[1],
        "se": (np.random.uniform(0.5, 1.6, (N, 1))).astype(np.float32),
        "sf": (np.random.uniform(0.5, 1.6, (N, 1))).astype(np.float32),
        "offs": striped(idx),
        "offs2": striped8(idx2),
        "offs3": striped8(idx3),
        "offs4": striped8(idx4),
        "offs5": striped8(idx5),
        "offs6": striped8(idx6),
        "offs7": striped8(idx7),
    }


def reference(xt_words, xt_scales, w_words, w_scales, w2_words, w2_scales, sa, sb, wb_words, wb_scales, se, sf, offs, offs2, offs3, offs4, offs5, offs6, offs7):
    idx = unstriped(offs)
    idx2 = unstriped8(offs2)
    idx3 = unstriped8(offs3)
    idx4 = unstriped8(offs4)
    idx5 = unstriped8(offs5)
    idx6 = unstriped8(offs6)
    idx7 = unstriped8(offs7)
    xtu = unpack_weight(xt_words, xt_scales, "e4m3")
    wu = unpack_weight(w_words, w_scales, "e2m1")
    w2u = unpack_weight(w2_words, w2_scales, "e4m3")
    wbu = unpack_weight(wb_words, wb_scales, "e4m3")
    xtidxg = xtu[:, idx]
    a = wu.T @ xtidxg
    b = w2u.T @ xtidxg
    hid = np.maximum(pick8(a, idx2, 64) * f64(sa), pick8(b, idx3, 64) * f64(sb))
    hidq = mxq(hid, 0, "e4m3")
    p = wbu.T @ hidq
    q1 = pick8(p, idx4, 16) * f64(se)
    q2 = pick8(p, idx5, 16) * f64(sf)
    lo = np.minimum(q1, q2)
    hi = np.maximum(q1, q2)
    m0 = np.zeros((N, U))
    m0[np.arange(N)[:, None], idx6[np.arange(N) % 128 // 16]] = lo
    m1 = np.zeros((N, U))
    m1[np.arange(N)[:, None], idx7[np.arange(N) % 128 // 16]] = hi
    y = m0 + m1
    return y

@@ -1,0 +1,223 @@
+from contextlib import ExitStack
+
+import concourse.mybir as mybir
+
+F32 = mybir.dt.float32
+BF16 = mybir.dt.bfloat16
+I32 = mybir.dt.int32
+U32 = mybir.dt.uint32
+U16 = mybir.dt.uint16
+U8 = mybir.dt.uint8
+E4M3X4 = mybir.dt.float8_e4m3fn_x4
+E2M1X4 = mybir.dt.float4_e2m1fn_x4
+COPY = mybir.ActivationFunctionType.Copy
+ALU = mybir.AluOpType
+
+P = 128
+PACK = 4
+K, J, R, T, O, N, E, U = 512, 512, 512, 1024, 256, 256, 128, 256
+FLOPS = 2 * (2 * K * R * J + R * N * O)
+
+
+def load_scale_rows(queue, plane, scales):
+    for q in range(4):
+        queue.dma_start(
+            out=plane[32 * q : 32 * q + 4, :].bitcast(I32),
+            in_=scales[0, 4 * q : 4 * q + 4, :].bitcast(I32),
+        )
+
+
+def tile_picked_tokens_plain_twin_groupmeet_one_endexchange_kernel(
+    tc, xt_words, xt_scales, w_words, w_scales, w2_words, w2_scales, sa, sb, wb_words, wb_scales,
+    se, sf, offs, offs2, offs3, offs4, offs5, offs6, offs7, out,
+):
+    nc = tc.nc
+    with ExitStack() as ctx:
+        lists = ctx.enter_context(tc.tile_pool(name="lists", bufs=1))
+        keep = ctx.enter_context(tc.tile_pool(name="keep", bufs=1))
+        psum = ctx.enter_context(tc.psum_pool(name="psum", bufs=1))
+
+        def load_list(src, name):
+            tile = lists.tile(list(src.shape), U16, name=name)
+            nc.sync.dma_start(tile[:], src)
+            return tile
+
+        def sb_tile(shape, dtype, name):
+            return keep.tile(shape, dtype, name=name, align_bytes=64)
+
+        def dealt(ap):
+            return ap.rearrange("p (t m) -> p t m", t=PACK)
+
+        def to_deal(ap):
+            return ap.rearrange("p (m t) -> p t m", t=PACK)
+
+        def bank_tile(index, width):
+            return psum.tile([P, width], F32, name=f"bank{index}")
+
+        xs_all = sb_tile([P, T], U8, "xs_all")
+        ws_raw = sb_tile([P, R], U8, "ws_raw")
+        w2s_raw = sb_tile([P, R], U8, "w2s_raw")
+        wbs = sb_tile([P, N], U8, "wbs")
+        nc.vector.memset(xs_all[:].bitcast(I32), 0)
+        nc.vector.memset(ws_raw[:].bitcast(I32), 0)
+        nc.vector.memset(w2s_raw[:].bitcast(I32), 0)
+        nc.vector.memset(wbs[:].bitcast(I32), 0)
+        pages = [[sb_tile([P, U], F32, f"page{s}{c}") for s in range(2)] for c in range(2)]
+        for c in range(2):
+            for s in range(2):
+                nc.vector.memset(pages[c][s][:], 0.0)
+
+        l1 = load_list(offs, "l1")
+        load_scale_rows(nc.scalar, xs_all, xt_scales)
+        xw_all = sb_tile([P, T], I32, "xw_all")
+        nc.sync.dma_start(out=xw_all[:], in_=xt_words[0].rearrange("p c b -> p (c b)").bitcast(I32))
+        ww_raw = sb_tile([P, R], U16, "ww_raw")
+        nc.sync.dma_start(out=ww_raw[:].bitcast(I32), in_=w_words[0].bitcast(I32))
+        w2w_raw = sb_tile([P, R], I32, "w2w_raw")
+        nc.sync.dma_start(out=w2w_raw[:], in_=w2_words[0].rearrange("p c b -> p (c b)").bitcast(I32))
+        load_scale_rows(nc.sync, ws_raw, w_scales)
+        l2 = load_list(offs2, "l2")
+        load_scale_rows(nc.sync, w2s_raw, w2_scales)
+        l3 = load_list(offs3, "l3")
+        sa_t = sb_tile([P, PACK], F32, "sa_t")
+        nc.gpsimd.dma_start(out=sa_t[:], in_=sa.rearrange("(p t) o -> p (t o)", t=PACK))
+        sb_t = sb_tile([P, PACK], F32, "sb_t")
+        nc.gpsimd.dma_start(out=sb_t[:], in_=sb.rearrange("(p t) o -> p (t o)", t=PACK))
+        wbw = sb_tile([P, N], I32, "wbw")
+        nc.sync.dma_start(out=wbw[:], in_=wb_words[0].rearrange("p c b -> p (c b)").bitcast(I32))
+        load_scale_rows(nc.sync, wbs, wb_scales)
+        l4 = load_list(offs4, "l4")
+        l5 = load_list(offs5, "l5")
+        se_t = sb_tile([P, 2], F32, "se_t")
+        sf_t = sb_tile([P, 2], F32, "sf_t")
+        with nc.allow_non_contiguous_dma(reason="one value a partition for each of the two output tiles"):
+            nc.sync.dma_start(out=se_t[:], in_=se.rearrange("(c p) o -> p (c o)", p=P))
+            nc.sync.dma_start(out=sf_t[:], in_=sf.rearrange("(c p) o -> p (c o)", p=P))
+        l6 = load_list(offs6, "l6")
+        l7 = load_list(offs7, "l7")
+
+        JH = J // 2
+        OH = O // 2
+        xs = sb_tile([P, J], U8, "xs")
+        nc.vector.tensor_copy(xs[:], xs_all[:].indirect(l1[:]))
+        xw = sb_tile([P, J], U32, "xw")
+        ww = sb_tile([P, R], U16, "ww")
+        nc.scalar.copy(dealt(ww[:]), to_deal(ww_raw[:]))
+        w2w = sb_tile([P, R], U32, "w2w")
+        nc.scalar.copy(dealt(w2w[:]), to_deal(w2w_raw[:].bitcast(U32)))
+        ws = [sb_tile([P, 2 * P], U8, f"ws{u}") for u in range(2)]
+        w2s = [sb_tile([P, P], U8, f"w2s{t}") for t in range(PACK)]
+
+        def gather_words(h):
+            nc.vector.tensor_copy(
+                xw[:, h * JH : (h + 1) * JH],
+                xw_all[:].bitcast(U32).indirect(l1[:, h * JH // 16 : (h + 1) * JH // 16]),
+            )
+
+        def deal_ws(u):
+            nc.vector.tensor_copy(
+                ws[u][:].rearrange("p (t m) -> p t m", t=2), to_deal(ws_raw[:])[:, 2 * u : 2 * u + 2, :]
+            )
+
+        gather_words(0)
+        deal_ws(0)
+        gather_words(1)
+        deal_ws(1)
+        for t in range(PACK):
+            nc.gpsimd.tensor_copy(w2s[t][:], to_deal(w2s_raw[:])[:, t, :])
+
+        def first_product(bank, which, t, cols):
+            m = slice(t * P, (t + 1) * P)
+            if which == "a":
+                lhs, plane = ww[:, m].bitcast(E2M1X4), ws[t // 2][:, (t % 2) * P : (t % 2 + 1) * P]
+            else:
+                lhs, plane = w2w[:, m].bitcast(E4M3X4), w2s[t][:]
+            nc.tensor.matmul_mx(
+                out=bank[:], lhsT=lhs, lhsT_scale=plane,
+                rhs=xw[:, cols].bitcast(E4M3X4), rhs_scale=xs[:, cols], start=True, stop=True,
+            )
+
+        rows = {(which, t): sb_tile([P, J], F32, f"rows_{which}{t}") for which in "ab" for t in range(PACK)}
+        ga = [sb_tile([P, 2, O], F32, f"ga{u}") for u in range(2)]
+        gb01 = sb_tile([P, 2, O], F32, "gb01")
+        gb23 = [sb_tile([P, 2, OH], F32, f"gb23_{h}") for h in range(2)]
+        hid = [sb_tile([P, OH, PACK], BF16, f"hid{h}") for h in range(2)]
+
+        for h in range(2):
+            cols = slice(h * JH, (h + 1) * JH)
+            for t in range(2):
+                bank = bank_tile(2 * h + t, JH)
+                first_product(bank, "a", t, cols)
+                if h == 0:
+                    nc.scalar.copy(rows["a", t][:, cols], bank[:])
+                else:
+                    nc.vector.tensor_copy(rows["a", t][:, cols], bank[:])
+        for i, (which, t) in enumerate([("a", 2), ("a", 3)] + [("b", t) for t in range(PACK)]):
+            bank = bank_tile((4 + i) % 8, J)
+            first_product(bank, which, t, slice(0, J))
+            nc.vector.tensor_copy(rows[which, t][:], bank[:])
+
+        for t in range(PACK):
+            nc.scalar.activation(
+                out=ga[t // 2][:, t % 2, :], in_=rows["a", t][:].indirect(l2[:]), func=COPY, scale=sa_t[:, t : t + 1]
+            )
+        for t in range(2):
+            nc.scalar.activation(
+                out=gb01[:, t, :], in_=rows["b", t][:].indirect(l3[:]), func=COPY, scale=sb_t[:, t : t + 1]
+            )
+        for h in range(2):
+            for t in range(2, PACK):
+                nc.scalar.activation(
+                    out=gb23[h][:, t - 2, :],
+                    in_=rows["b", t][:].indirect(l3[:, h * OH // 16 : (h + 1) * OH // 16]),
+                    func=COPY, scale=sb_t[:, t : t + 1],
+                )
+
+        for h in range(2):
+            cols = slice(h * OH, (h + 1) * OH)
+            nc.vector.tensor_tensor(
+                hid[h][:, :, 0:2], ga[0][:, :, cols].rearrange("p t o -> p o t"),
+                gb01[:, :, cols].rearrange("p t o -> p o t"), ALU.max,
+            )
+
+        prow = [sb_tile([P, O], F32, f"prow{c}") for c in range(2)]
+        for h in range(2):
+            cols = slice(h * OH, (h + 1) * OH)
+            nc.vector.tensor_tensor(
+                hid[h][:, :, 2:4], ga[1][:, :, cols].rearrange("p t o -> p o t"),
+                gb23[h][:].rearrange("p t o -> p o t"), ALU.max,
+            )
+            hw = sb_tile([P, OH], U32, f"hw{h}")
+            hs = sb_tile([P, OH], U8, f"hs{h}")
+            nc.vector.quantize_mx(out=hw[:].bitcast(E4M3X4), scales=hs[:], in_=hid[h][:].rearrange("p o t -> p (o t)"))
+            for c in range(2):
+                m = slice(c * P, (c + 1) * P)
+                bank = bank_tile(2 + 2 * h + c, OH)
+                nc.tensor.matmul_mx(
+                    out=bank[:], lhsT=wbw[:, m].bitcast(E4M3X4), lhsT_scale=wbs[:, m],
+                    rhs=hw[:].bitcast(E4M3X4), rhs_scale=hs[:], start=True, stop=True,
+                )
+                if h == 1 and c == 1:
+                    nc.vector.tensor_copy(prow[c][:, cols], bank[:])
+                else:
+                    nc.scalar.copy(prow[c][:, cols], bank[:])
+
+        picked = []
+        for c in range(2):
+            q1 = sb_tile([P, E], F32, f"q1_{c}")
+            q2 = sb_tile([P, E], F32, f"q2_{c}")
+            nc.scalar.activation(out=q1[:], in_=prow[c][:].indirect(l4[:]), func=COPY, scale=se_t[:, c : c + 1])
+            nc.scalar.activation(out=q2[:], in_=prow[c][:].indirect(l5[:]), func=COPY, scale=sf_t[:, c : c + 1])
+            lo = sb_tile([P, E], F32, f"lo{c}")
+            hi = sb_tile([P, E], F32, f"hi{c}")
+            nc.vector.tensor_tensor(lo[:], q1[:], q2[:], ALU.min)
+            nc.vector.tensor_tensor(hi[:], q1[:], q2[:], ALU.max)
+            picked.append((lo, hi))
+
+        for c in range(2):
+            lo, hi = picked[c]
+            nc.scalar.activation(out=pages[c][0][:].indirect(l6[:]), in_=lo[:], func=COPY)
+            nc.scalar.activation(out=pages[c][1][:].indirect(l7[:]), in_=hi[:], func=COPY)
+            total = sb_tile([P, U], F32, f"total{c}")
+            nc.vector.tensor_tensor(total[:], pages[c][0][:], pages[c][1][:], ALU.add)
+            nc.sync.dma_start(out=out[c * P : (c + 1) * P, :], in_=total[:])

@@ -19,11 +19,11 @@ K, J, R, T, O, N, E, U = 512, 512, 512, 1024, 256, 256, 128, 256
 FLOPS = 2 * (2 * K * R * J + R * N * O)
 
 
-def load_scale_rows(queue, plane, scales):
+def load_scale_rows(queues, plane, scales):
     for q in range(4):
-        queue.dma_start(
-            out=plane[32 * q : 32 * q + 4, :].bitcast(I32),
-            in_=scales[0, 4 * q : 4 * q + 4, :].bitcast(I32),
+        queues[q].dma_start(
+            out=plane[32 * q : 32 * q + 32, :].bitcast(I32),
+            in_=scales[0, 4 * q : 4 * q + 4, :].bitcast(I32).partition_broadcast(8),
         )
 
 
@@ -58,26 +58,24 @@ def tile_picked_tokens_plain_twin_groupmeet_one_endexchange_kernel(
         ws_raw = sb_tile([P, R], U8, "ws_raw")
         w2s_raw = sb_tile([P, R], U8, "w2s_raw")
         wbs = sb_tile([P, N], U8, "wbs")
-        nc.vector.memset(xs_all[:].bitcast(I32), 0)
-        nc.vector.memset(ws_raw[:].bitcast(I32), 0)
-        nc.vector.memset(w2s_raw[:].bitcast(I32), 0)
-        nc.vector.memset(wbs[:].bitcast(I32), 0)
         pages = [[sb_tile([P, U], F32, f"page{s}{c}") for s in range(2)] for c in range(2)]
         for c in range(2):
             for s in range(2):
                 nc.vector.memset(pages[c][s][:], 0.0)
 
+        nc.vector.memset(ws_raw[:].bitcast(I32), 0)
+        ws_rows = sb_tile([4, 4, R // 4], I32, "ws_rows")
+        nc.scalar.dma_start(out=ws_rows[:], in_=w_scales[0].bitcast(I32).rearrange("(q r) c -> r q c", r=4))
         l1 = load_list(offs, "l1")
-        load_scale_rows(nc.scalar, xs_all, xt_scales)
+        load_scale_rows([nc.scalar, nc.scalar, nc.sync, nc.sync], xs_all, xt_scales)
         xw_all = sb_tile([P, T], I32, "xw_all")
         nc.sync.dma_start(out=xw_all[:], in_=xt_words[0].rearrange("p c b -> p (c b)").bitcast(I32))
         ww_raw = sb_tile([P, R], U16, "ww_raw")
         nc.sync.dma_start(out=ww_raw[:].bitcast(I32), in_=w_words[0].bitcast(I32))
         w2w_raw = sb_tile([P, R], I32, "w2w_raw")
         nc.sync.dma_start(out=w2w_raw[:], in_=w2_words[0].rearrange("p c b -> p (c b)").bitcast(I32))
-        load_scale_rows(nc.sync, ws_raw, w_scales)
         l2 = load_list(offs2, "l2")
-        load_scale_rows(nc.sync, w2s_raw, w2_scales)
+        load_scale_rows([nc.sync] * 4, w2s_raw, w2_scales)
         l3 = load_list(offs3, "l3")
         sa_t = sb_tile([P, PACK], F32, "sa_t")
         nc.gpsimd.dma_start(out=sa_t[:], in_=sa.rearrange("(p t) o -> p (t o)", t=PACK))
@@ -85,7 +83,7 @@ def tile_picked_tokens_plain_twin_groupmeet_one_endexchange_kernel(
         nc.gpsimd.dma_start(out=sb_t[:], in_=sb.rearrange("(p t) o -> p (t o)", t=PACK))
         wbw = sb_tile([P, N], I32, "wbw")
         nc.sync.dma_start(out=wbw[:], in_=wb_words[0].rearrange("p c b -> p (c b)").bitcast(I32))
-        load_scale_rows(nc.sync, wbs, wb_scales)
+        load_scale_rows([nc.sync] * 4, wbs, wb_scales)
         l4 = load_list(offs4, "l4")
         l5 = load_list(offs5, "l5")
         se_t = sb_tile([P, 2], F32, "se_t")
@@ -119,6 +117,8 @@ def tile_picked_tokens_plain_twin_groupmeet_one_endexchange_kernel(
                 ws[u][:].rearrange("p (t m) -> p t m", t=2), to_deal(ws_raw[:])[:, 2 * u : 2 * u + 2, :]
             )
 
+        for q in range(4):
+            nc.vector.tensor_copy(ws_raw[32 * q : 32 * q + 4, :].bitcast(I32), ws_rows[:, q, :])
         gather_words(0)
         deal_ws(0)
         gather_words(1)
@@ -187,6 +187,8 @@ def tile_picked_tokens_plain_twin_groupmeet_one_endexchange_kernel(
                 hid[h][:, :, 2:4], ga[1][:, :, cols].rearrange("p t o -> p o t"),
                 gb23[h][:].rearrange("p t o -> p o t"), ALU.max,
             )
+        for h in range(2):
+            cols = slice(h * OH, (h + 1) * OH)
             hw = sb_tile([P, OH], U32, f"hw{h}")
             hs = sb_tile([P, OH], U8, f"hs{h}")
             nc.vector.quantize_mx(out=hw[:].bitcast(E4M3X4), scales=hs[:], in_=hid[h][:].rearrange("p o t -> p (o t)"))

from contextlib import ExitStack

import concourse.mybir as mybir

F32 = mybir.dt.float32
BF16 = mybir.dt.bfloat16
I32 = mybir.dt.int32
U32 = mybir.dt.uint32
U16 = mybir.dt.uint16
U8 = mybir.dt.uint8
E4M3X4 = mybir.dt.float8_e4m3fn_x4
E2M1X4 = mybir.dt.float4_e2m1fn_x4
COPY = mybir.ActivationFunctionType.Copy
ALU = mybir.AluOpType

P = 128
PACK = 4
K, J, R, T, O, N, E, U = 512, 512, 512, 1024, 256, 256, 128, 256
FLOPS = 2 * (2 * K * R * J + R * N * O)


def load_scale_rows(queues, plane, scales):
    for q in range(4):
        queues[q].dma_start(
            out=plane[32 * q : 32 * q + 32, :].bitcast(I32),
            in_=scales[0, 4 * q : 4 * q + 4, :].bitcast(I32).partition_broadcast(8),
        )


def tile_picked_tokens_plain_twin_groupmeet_one_endexchange_kernel(
    tc, xt_words, xt_scales, w_words, w_scales, w2_words, w2_scales, sa, sb, wb_words, wb_scales,
    se, sf, offs, offs2, offs3, offs4, offs5, offs6, offs7, out,
):
    nc = tc.nc
    with ExitStack() as ctx:
        lists = ctx.enter_context(tc.tile_pool(name="lists", bufs=1))
        keep = ctx.enter_context(tc.tile_pool(name="keep", bufs=1))
        psum = ctx.enter_context(tc.psum_pool(name="psum", bufs=1))

        def load_list(src, name):
            tile = lists.tile(list(src.shape), U16, name=name)
            nc.sync.dma_start(tile[:], src)
            return tile

        def sb_tile(shape, dtype, name):
            return keep.tile(shape, dtype, name=name, align_bytes=64)

        def dealt(ap):
            return ap.rearrange("p (t m) -> p t m", t=PACK)

        def to_deal(ap):
            return ap.rearrange("p (m t) -> p t m", t=PACK)

        def bank_tile(index, width):
            return psum.tile([P, width], F32, name=f"bank{index}")

        xs_all = sb_tile([P, T], U8, "xs_all")
        ws_raw = sb_tile([P, R], U8, "ws_raw")
        w2s_raw = sb_tile([P, R], U8, "w2s_raw")
        wbs = sb_tile([P, N], U8, "wbs")
        pages = [[sb_tile([P, U], F32, f"page{s}{c}") for s in range(2)] for c in range(2)]
        for c in range(2):
            for s in range(2):
                nc.vector.memset(pages[c][s][:], 0.0)

        nc.vector.memset(ws_raw[:].bitcast(I32), 0)
        ws_rows = sb_tile([4, 4, R // 4], I32, "ws_rows")
        nc.scalar.dma_start(out=ws_rows[:], in_=w_scales[0].bitcast(I32).rearrange("(q r) c -> r q c", r=4))
        l1 = load_list(offs, "l1")
        load_scale_rows([nc.scalar, nc.scalar, nc.sync, nc.sync], xs_all, xt_scales)
        xw_all = sb_tile([P, T], I32, "xw_all")
        nc.sync.dma_start(out=xw_all[:], in_=xt_words[0].rearrange("p c b -> p (c b)").bitcast(I32))
        ww_raw = sb_tile([P, R], U16, "ww_raw")
        nc.sync.dma_start(out=ww_raw[:].bitcast(I32), in_=w_words[0].bitcast(I32))
        w2w_raw = sb_tile([P, R], I32, "w2w_raw")
        nc.sync.dma_start(out=w2w_raw[:], in_=w2_words[0].rearrange("p c b -> p (c b)").bitcast(I32))
        l2 = load_list(offs2, "l2")
        load_scale_rows([nc.sync] * 4, w2s_raw, w2_scales)
        l3 = load_list(offs3, "l3")
        sa_t = sb_tile([P, PACK], F32, "sa_t")
        nc.gpsimd.dma_start(out=sa_t[:], in_=sa.rearrange("(p t) o -> p (t o)", t=PACK))
        sb_t = sb_tile([P, PACK], F32, "sb_t")
        nc.gpsimd.dma_start(out=sb_t[:], in_=sb.rearrange("(p t) o -> p (t o)", t=PACK))
        wbw = sb_tile([P, N], I32, "wbw")
        nc.sync.dma_start(out=wbw[:], in_=wb_words[0].rearrange("p c b -> p (c b)").bitcast(I32))
        load_scale_rows([nc.sync] * 4, wbs, wb_scales)
        l4 = load_list(offs4, "l4")
        l5 = load_list(offs5, "l5")
        se_t = sb_tile([P, 2], F32, "se_t")
        sf_t = sb_tile([P, 2], F32, "sf_t")
        with nc.allow_non_contiguous_dma(reason="one value a partition for each of the two output tiles"):
            nc.sync.dma_start(out=se_t[:], in_=se.rearrange("(c p) o -> p (c o)", p=P))
            nc.sync.dma_start(out=sf_t[:], in_=sf.rearrange("(c p) o -> p (c o)", p=P))
        l6 = load_list(offs6, "l6")
        l7 = load_list(offs7, "l7")

        JH = J // 2
        OH = O // 2
        xs = sb_tile([P, J], U8, "xs")
        nc.vector.tensor_copy(xs[:], xs_all[:].indirect(l1[:]))
        xw = sb_tile([P, J], U32, "xw")
        ww = sb_tile([P, R], U16, "ww")
        nc.scalar.copy(dealt(ww[:]), to_deal(ww_raw[:]))
        w2w = sb_tile([P, R], U32, "w2w")
        nc.scalar.copy(dealt(w2w[:]), to_deal(w2w_raw[:].bitcast(U32)))
        ws = [sb_tile([P, 2 * P], U8, f"ws{u}") for u in range(2)]
        w2s = [sb_tile([P, P], U8, f"w2s{t}") for t in range(PACK)]

        def gather_words(h):
            nc.vector.tensor_copy(
                xw[:, h * JH : (h + 1) * JH],
                xw_all[:].bitcast(U32).indirect(l1[:, h * JH // 16 : (h + 1) * JH // 16]),
            )

        def deal_ws(u):
            nc.vector.tensor_copy(
                ws[u][:].rearrange("p (t m) -> p t m", t=2), to_deal(ws_raw[:])[:, 2 * u : 2 * u + 2, :]
            )

        for q in range(4):
            nc.vector.tensor_copy(ws_raw[32 * q : 32 * q + 4, :].bitcast(I32), ws_rows[:, q, :])
        gather_words(0)
        deal_ws(0)
        gather_words(1)
        deal_ws(1)
        for t in range(PACK):
            nc.gpsimd.tensor_copy(w2s[t][:], to_deal(w2s_raw[:])[:, t, :])

        def first_product(bank, which, t, cols):
            m = slice(t * P, (t + 1) * P)
            if which == "a":
                lhs, plane = ww[:, m].bitcast(E2M1X4), ws[t // 2][:, (t % 2) * P : (t % 2 + 1) * P]
            else:
                lhs, plane = w2w[:, m].bitcast(E4M3X4), w2s[t][:]
            nc.tensor.matmul_mx(
                out=bank[:], lhsT=lhs, lhsT_scale=plane,
                rhs=xw[:, cols].bitcast(E4M3X4), rhs_scale=xs[:, cols], start=True, stop=True,
            )

        rows = {(which, t): sb_tile([P, J], F32, f"rows_{which}{t}") for which in "ab" for t in range(PACK)}
        ga = [sb_tile([P, 2, O], F32, f"ga{u}") for u in range(2)]
        gb01 = sb_tile([P, 2, O], F32, "gb01")
        gb23 = [sb_tile([P, 2, OH], F32, f"gb23_{h}") for h in range(2)]
        hid = [sb_tile([P, OH, PACK], BF16, f"hid{h}") for h in range(2)]

        for h in range(2):
            cols = slice(h * JH, (h + 1) * JH)
            for t in range(2):
                bank = bank_tile(2 * h + t, JH)
                first_product(bank, "a", t, cols)
                if h == 0:
                    nc.scalar.copy(rows["a", t][:, cols], bank[:])
                else:
                    nc.vector.tensor_copy(rows["a", t][:, cols], bank[:])
        for i, (which, t) in enumerate([("a", 2), ("a", 3)] + [("b", t) for t in range(PACK)]):
            bank = bank_tile((4 + i) % 8, J)
            first_product(bank, which, t, slice(0, J))
            nc.vector.tensor_copy(rows[which, t][:], bank[:])

        for t in range(PACK):
            nc.scalar.activation(
                out=ga[t // 2][:, t % 2, :], in_=rows["a", t][:].indirect(l2[:]), func=COPY, scale=sa_t[:, t : t + 1]
            )
        for t in range(2):
            nc.scalar.activation(
                out=gb01[:, t, :], in_=rows["b", t][:].indirect(l3[:]), func=COPY, scale=sb_t[:, t : t + 1]
            )
        for h in range(2):
            for t in range(2, PACK):
                nc.scalar.activation(
                    out=gb23[h][:, t - 2, :],
                    in_=rows["b", t][:].indirect(l3[:, h * OH // 16 : (h + 1) * OH // 16]),
                    func=COPY, scale=sb_t[:, t : t + 1],
                )

        for h in range(2):
            cols = slice(h * OH, (h + 1) * OH)
            nc.vector.tensor_tensor(
                hid[h][:, :, 0:2], ga[0][:, :, cols].rearrange("p t o -> p o t"),
                gb01[:, :, cols].rearrange("p t o -> p o t"), ALU.max,
            )

        prow = [sb_tile([P, O], F32, f"prow{c}") for c in range(2)]
        for h in range(2):
            cols = slice(h * OH, (h + 1) * OH)
            nc.vector.tensor_tensor(
                hid[h][:, :, 2:4], ga[1][:, :, cols].rearrange("p t o -> p o t"),
                gb23[h][:].rearrange("p t o -> p o t"), ALU.max,
            )
        for h in range(2):
            cols = slice(h * OH, (h + 1) * OH)
            hw = sb_tile([P, OH], U32, f"hw{h}")
            hs = sb_tile([P, OH], U8, f"hs{h}")
            nc.vector.quantize_mx(out=hw[:].bitcast(E4M3X4), scales=hs[:], in_=hid[h][:].rearrange("p o t -> p (o t)"))
            for c in range(2):
                m = slice(c * P, (c + 1) * P)
                bank = bank_tile(2 + 2 * h + c, OH)
                nc.tensor.matmul_mx(
                    out=bank[:], lhsT=wbw[:, m].bitcast(E4M3X4), lhsT_scale=wbs[:, m],
                    rhs=hw[:].bitcast(E4M3X4), rhs_scale=hs[:], start=True, stop=True,
                )
                if h == 1 and c == 1:
                    nc.vector.tensor_copy(prow[c][:, cols], bank[:])
                else:
                    nc.scalar.copy(prow[c][:, cols], bank[:])

        picked = []
        for c in range(2):
            q1 = sb_tile([P, E], F32, f"q1_{c}")
            q2 = sb_tile([P, E], F32, f"q2_{c}")
            nc.scalar.activation(out=q1[:], in_=prow[c][:].indirect(l4[:]), func=COPY, scale=se_t[:, c : c + 1])
            nc.scalar.activation(out=q2[:], in_=prow[c][:].indirect(l5[:]), func=COPY, scale=sf_t[:, c : c + 1])
            lo = sb_tile([P, E], F32, f"lo{c}")
            hi = sb_tile([P, E], F32, f"hi{c}")
            nc.vector.tensor_tensor(lo[:], q1[:], q2[:], ALU.min)
            nc.vector.tensor_tensor(hi[:], q1[:], q2[:], ALU.max)
            picked.append((lo, hi))

        for c in range(2):
            lo, hi = picked[c]
            nc.scalar.activation(out=pages[c][0][:].indirect(l6[:]), in_=lo[:], func=COPY)
            nc.scalar.activation(out=pages[c][1][:].indirect(l7[:]), in_=hi[:], func=COPY)
            total = sb_tile([P, U], F32, f"total{c}")
            nc.vector.tensor_tensor(total[:], pages[c][0][:], pages[c][1][:], ALU.add)
            nc.sync.dma_start(out=out[c * P : (c + 1) * P, :], in_=total[:])
